import numpy as np
import ml_dtypes


def mxq(x, axis, fmt="e4m3"):
    dtype, down = {"e4m3": (ml_dtypes.float8_e4m3fn, 7), "e5m2": (ml_dtypes.float8_e5m2, 14)}[fmt]
    v = np.moveaxis(np.asarray(x, np.float32).astype(ml_dtypes.bfloat16).astype(np.float64), axis, -1)
    blocks = v.reshape(v.shape[:-1] + (-1, 32))
    amax = np.abs(blocks).max(-1, keepdims=True)
    byte = np.maximum(np.where(amax > 0, np.frexp(amax)[1] - 1 + 127, 0) - down, 1)
    scale = np.exp2(byte - 127.0)
    codes = (blocks / scale).astype(np.float32).astype(dtype).astype(np.float64)
    return np.moveaxis((codes * scale).reshape(v.shape), -1, axis)


WIDE = False


def mx_kscale(k):
    if not WIDE:
        return np.ones(k)
    levels = np.array([30, -30])
    if k % 512:
        return np.exp2(np.random.permutation(np.resize(levels, k // 32))).repeat(32)
    a = np.empty((k // 512, 16))
    for p in range(k // 512):
        a[p, :8] = np.random.permutation(np.resize(levels, 8))
        for g in range(8):
            far = levels[np.abs(levels - a[p, g]) >= 10]
            a[p, g + 8] = far[np.random.randint(len(far))]
    return np.exp2(a.ravel()).repeat(32)


def f64(x):
    return np.asarray(x).astype(np.float64)


E2M1 = np.array([0.0, 0.5, 1.0, 1.5, 2.0, 3.0, 4.0, 6.0, -0.0, -0.5, -1.0, -1.5, -2.0, -3.0, -4.0, -6.0])


def pack_weight(w, fmt):
    k, n = w.shape
    w = f64(np.asarray(w, np.float32).astype(ml_dtypes.bfloat16)).reshape(k // 32, 32, n)
    amax = np.abs(w).max(1)
    if fmt == "e4m3":
        byte = np.frexp(amax)[1] - 1 + 127 - 7
    else:
        mant, ex = np.frexp(amax / 6.0)
        byte = np.where(mant > 0.5, ex, ex - 1) + 127
    byte = np.clip(np.where(amax > 0, byte, 1), 1, 254)
    scaled = (w * np.exp2(127.0 - byte)[:, None, :]).reshape(k, n).astype(np.float32)
    by_word = np.ascontiguousarray(scaled.reshape(k // 512, 128, 4, n).transpose(0, 1, 3, 2))
    if fmt == "e4m3":
        words = by_word.astype(ml_dtypes.float8_e4m3fn).view(np.uint8)
    else:
        c = by_word.astype(ml_dtypes.float4_e2m1fn).view(np.uint8) & 0xF
        words = (c[..., 0::2] | (c[..., 1::2] << 4)).reshape(k // 512, 128, 2 * n)
    return np.ascontiguousarray(words), np.ascontiguousarray(byte.astype(np.uint8).reshape(k // 512, 16, n))


def unpack_weight(words, scales, fmt):
    g, _, n = scales.shape
    words = np.ascontiguousarray(words).reshape(g, 128, n, -1)
    if fmt == "e4m3":
        vals = words.view(ml_dtypes.float8_e4m3fn).astype(np.float64)
    else:
        nib = np.empty((g, 128, n, 4), np.uint8)
        nib[..., 0::2] = words & 0xF
        nib[..., 1::2] = words >> 4
        vals = E2M1[nib]
    vals = vals * np.repeat(np.exp2(scales.astype(np.float64) - 127.0), 8, axis=1)[..., None]
    return vals.transpose(0, 1, 3, 2).reshape(g * 512, n)


def planes(y):
    n, m = y.shape
    v = y.astype(np.float32).astype(ml_dtypes.bfloat16).astype(np.float64).reshape(n // 32, 32, m)
    top = np.abs(v).max(1)
    byte = np.clip(np.where(top > 0, np.frexp(top)[1] - 1 + 127 - 7, 1), 1, 254)
    codes = (v * np.exp2(127.0 - byte)[:, None, :]).reshape(n, m).astype(np.float32).astype(ml_dtypes.float8_e4m3fn).view(np.uint8)
    words = codes.reshape(n // 512, 128, 4, m).transpose(0, 1, 3, 2)
    return np.ascontiguousarray(words), np.ascontiguousarray(byte.astype(np.uint8).reshape(n // 512, 16, m))


O, K, M, T = 1024, 2048, 1024, 1024


def setup_inputs():
    n = np.random.standard_normal
    s = mx_kscale(K)[:, None]
    dy = np.exp(0.5 * n((1, T))) * n((K, T))
    w = n((K, M)) / np.sqrt(K) / s
    p_w8 = pack_weight(w[:O], "e4m3")
    p_w4 = pack_weight(w[O:], "e2m1")
    return {
        "dy": (dy * s).astype(np.float32),
        "w8_words": p_w8[0],
        "w8_scales": p_w8[1],
        "w4_words": p_w4[0],
        "w4_scales": p_w4[1],
        "r": (n((1024, 1024))).astype(np.float32),
    }


def reference(dy, w8_words, w8_scales, w4_words, w4_scales, r):
    dy_ = mxq(f64(dy), 0, "e5m2")
    w8_ = unpack_weight(w8_words, w8_scales, "e4m3")
    w4_ = unpack_weight(w4_words, w4_scales, "e2m1")
    y = w8_.T @ dy_[:O] + w4_.T @ dy_[O:]
    out_0 = f64(r) + y
    return (out_0,) + planes(out_0)

@@ -1,0 +1,207 @@
+from contextlib import ExitStack
+
+import concourse.mybir as mybir
+
+O, K, M, T = 1024, 2048, 1024, 1024
+FLOPS = 2 * K * M * T
+
+F32 = mybir.dt.float32
+BF16 = mybir.dt.bfloat16
+I32 = mybir.dt.int32
+U32 = mybir.dt.uint32
+U8 = mybir.dt.uint8
+E4M3 = mybir.dt.float8_e4m3fn_x4
+E5M2 = mybir.dt.float8_e5m2_x4
+E2M1 = mybir.dt.float4_e2m1fn_x4
+
+P = 128
+PACK = 4
+K_PASS = P * PACK
+N = 512
+PASSES = K // K_PASS
+W_PASSES = O // K_PASS
+BLOCKS = M // K_PASS
+HALVES = T // N
+RUN = 4
+VECTOR_COLS = 288
+
+
+def interleave(copy, grouped, rows, c0, c1, g0, run):
+    copy(
+        out=grouped[:, c0 - g0 : c1 - g0, :].rearrange("p (c i) j -> p c j i", i=run),
+        in_=rows[:, :, c0:c1].rearrange("p j (c i) -> p c j i", i=run),
+    )
+
+
+def tile_mix_dyq_fm_pl_res_kernel(
+    tc, dy, w8_words, w8_scales, w4_words, w4_scales, r, out_0, out_1, out_2
+):
+    nc = tc.nc
+    with ExitStack() as ctx:
+        keep = ctx.enter_context(tc.tile_pool(name="keep", bufs=1))
+        stage = ctx.enter_context(tc.tile_pool(name="stage", bufs=4))
+        psum = ctx.enter_context(tc.psum_pool(name="psum", bufs=1))
+        ctx.enter_context(tc.manual_schedule())
+
+        w8_raw = keep.tile([P, W_PASSES, M], I32, align_bytes=64)
+        w4_raw = keep.tile([P, W_PASSES, 2 * M], U8, align_bytes=64)
+        s8_raw = keep.tile([P, W_PASSES, M], U8, align_bytes=64)
+        s4_raw = keep.tile([P, W_PASSES, M], U8, align_bytes=64)
+        w8 = keep.tile([P, W_PASSES * M], U32, align_bytes=64)
+        w4 = keep.tile([P, W_PASSES * 2 * M], U8, align_bytes=64)
+        s8 = keep.tile([P, W_PASSES * M], U8, align_bytes=64)
+        s4 = keep.tile([P, W_PASSES * M], U8, align_bytes=64)
+        dy_raw = [keep.tile([P, PACK, T], F32, name="dy_raw%d" % g, align_bytes=64) for g in range(PASSES)]
+        res = [keep.tile([P, PACK, T], F32, name="res%d" % a, align_bytes=64) for a in range(BLOCKS)]
+        dy_codes = {}
+        dy_scales = {}
+        for g in range(PASSES):
+            for h in range(HALVES):
+                dy_codes[g, h] = keep.tile([P, N], U32, name="dy_codes%d%d" % (g, h), align_bytes=64)
+                dy_scales[g, h] = keep.tile([P, N], U8, name="dy_scales%d%d" % (g, h), align_bytes=64)
+        out_codes = [keep.tile([P, T], U32, name="out_codes%d" % a, align_bytes=64) for a in range(BLOCKS)]
+        out_scales = keep.tile([P, T], U8, align_bytes=64)
+
+        def load_scales(raw, scales):
+            rows = scales.bitcast(I32).rearrange("a (q j) n -> j q a n", j=4)
+            for j in range(4):
+                nc.sync.dma_start(out=raw[j:P:32, :, :].bitcast(I32), in_=rows[j])
+
+        def load_dy(g):
+            rows = dy[g * K_PASS : (g + 1) * K_PASS, :]
+            nc.sync.dma_start(out=dy_raw[g][:], in_=rows.rearrange("(p j) t -> p j t", j=PACK))
+
+        def rows_of(x, a):
+            return x[a * K_PASS : (a + 1) * K_PASS, :].rearrange("(p j) t -> p j t", j=PACK)
+
+        nc.vector.memset(s8_raw[:].bitcast(I32), 0)
+        nc.vector.memset(s4_raw[:].bitcast(I32), 0)
+
+        nc.sync.dma_start(out=w8_raw[:], in_=w8_words.rearrange("a p n i -> p a (n i)").bitcast(I32))
+        load_scales(s8_raw, w8_scales)
+        load_dy(0)
+        nc.sync.dma_start(out=w4_raw[:].bitcast(I32), in_=w4_words.rearrange("a p n -> p a n").bitcast(I32))
+        load_scales(s4_raw, w4_scales)
+        for g in range(1, PASSES):
+            load_dy(g)
+        for a in range(BLOCKS):
+            for j in (0, 2):
+                nc.sync.dma_start(out=res[a][:, j : j + 2, :], in_=rows_of(r, a)[:, j : j + 2, :])
+
+        def deal_w8():
+            nc.vector.tensor_copy(
+                out=w8[:].bitcast(I32).rearrange("p (b j c i) -> p b c j i", j=PACK, i=RUN, c=P // RUN),
+                in_=w8_raw[:].rearrange("p a (b c i j) -> p (a b) c j i", j=PACK, i=RUN, c=P // RUN),
+            )
+
+        def deal_w4():
+            nc.vector.tensor_copy(
+                out=w4[:].rearrange("p (b j m e) -> p b j m e", j=PACK, m=P, e=2),
+                in_=w4_raw[:].rearrange("p a (b m j e) -> p (a b) j m e", j=PACK, m=P, e=2),
+            )
+
+        def deal_scales(dealt, raw):
+            nc.vector.tensor_copy(
+                out=dealt[:].rearrange("p (b j m) -> p b j m", j=PACK, m=P),
+                in_=raw[:].rearrange("p a (b m j) -> p (a b) j m", j=PACK, m=P),
+            )
+
+        def round_half(rows, h, vector_cols, run):
+            grouped = stage.tile([P, N, PACK], BF16, name="grouped", align_bytes=64)
+            c0 = h * N
+            if vector_cols > 0:
+                interleave(nc.vector.tensor_copy, grouped, rows, c0, c0 + vector_cols, c0, run)
+            interleave(nc.scalar.copy, grouped, rows, c0 + vector_cols, c0 + N, c0, run)
+            return grouped
+
+        def quantize_dy(g):
+            grouped = [round_half(dy_raw[g], h, VECTOR_COLS, RUN) for h in range(HALVES)]
+            for h in range(HALVES):
+                nc.vector.quantize_mx(
+                    out=dy_codes[g, h][:].bitcast(E5M2),
+                    scales=dy_scales[g, h][:],
+                    in_=grouped[h][:].rearrange("p c j -> p (c j)"),
+                )
+
+        def multiply(bank, a, j, h, g):
+            col = (g % W_PASSES) * M + a * K_PASS + j * P
+            if g < W_PASSES:
+                lhsT = w8[:, col : col + P].bitcast(E4M3)
+                lhsT_scale = s8[:, col : col + P]
+            else:
+                lhsT = w4[:, 2 * col : 2 * (col + P)].bitcast(E2M1)
+                lhsT_scale = s4[:, col : col + P]
+            nc.tensor.matmul_mx(
+                out=bank[:],
+                lhsT=lhsT,
+                lhsT_scale=lhsT_scale,
+                rhs=dy_codes[g, h][:].bitcast(E5M2),
+                rhs_scale=dy_scales[g, h][:],
+                start=(g == 0),
+                stop=(g == PASSES - 1),
+            )
+
+        def add_residual(bank, a, j, h):
+            part = res[a][:, j, h * N : (h + 1) * N]
+            nc.vector.tensor_tensor(out=part, in0=bank[:], in1=part, op=mybir.AluOpType.add)
+
+        def quantize_out(grouped, a, h):
+            nc.vector.quantize_mx(
+                out=out_codes[a][:, h * N : (h + 1) * N].bitcast(E4M3),
+                scales=out_scales[4 * a : P, h * N : (h + 1) * N],
+                in_=grouped[:].rearrange("p c j -> p (c j)"),
+            )
+
+        def store_rows(a, j):
+            nc.sync.dma_start(out=rows_of(out_0, a)[:, j : j + 2, :], in_=res[a][:, j : j + 2, :])
+
+        def store_codes(a):
+            nc.sync.dma_start(
+                out=out_1[a].rearrange("p n i -> p (n i)").bitcast(I32), in_=out_codes[a][:].bitcast(I32)
+            )
+
+        groups = [(j, h) for h in range(HALVES) for j in range(PACK)]
+
+        deal_w8()
+        deal_scales(s8, s8_raw)
+        banks = [psum.tile([P, N], F32, name="bank%d" % n) for n in range(len(groups))]
+        for g in range(PASSES):
+            quantize_dy(g)
+            if g == 0:
+                deal_w4()
+                deal_scales(s4, s4_raw)
+            for n, (j, h) in enumerate(groups):
+                multiply(banks[n], 0, j, h, g)
+
+        grouped = {}
+        later = []
+        for n, (j, h) in enumerate(groups):
+            add_residual(banks[n], 0, j, h)
+            if j == PACK - 1:
+                grouped[0, h] = round_half(res[0], h, 0, 1)
+            if h == HALVES - 1 and j % 2 == 1:
+                store_rows(0, j - 1)
+            bank = psum.tile([P, N], F32, name="bank%d" % n)
+            later.append(bank)
+            for g in range(PASSES):
+                multiply(bank, 1, j, h, g)
+
+        for n, (j, h) in enumerate(groups):
+            add_residual(later[n], 1, j, h)
+            if n == 3:
+                grouped[1, 0] = round_half(res[1], 0, 0, 1)
+                quantize_out(grouped[0, 0], 0, 0)
+            if n == 4:
+                quantize_out(grouped[0, 1], 0, 1)
+                store_codes(0)
+            if h == HALVES - 1 and j % 2 == 1:
+                store_rows(1, j - 1)
+        grouped[1, 1] = round_half(res[1], 1, 352, 1)
+        quantize_out(grouped[1, 0], 1, 0)
+        quantize_out(grouped[1, 1], 1, 1)
+        for q in (0, 2, 1, 3):
+            nc.sync.dma_start(
+                out=out_2[:, 4 * q : 4 * q + 4, :].bitcast(I32),
+                in_=out_scales[32 * q : 32 * q + 8, :].bitcast(I32),
+            )
+        store_codes(1)

@@ -51,7 +51,8 @@ def tile_mix_dyq_fm_pl_res_kernel(
         w4 = keep.tile([P, W_PASSES * 2 * M], U8, align_bytes=64)
         s8 = keep.tile([P, W_PASSES * M], U8, align_bytes=64)
         s4 = keep.tile([P, W_PASSES * M], U8, align_bytes=64)
-        dy_raw = [keep.tile([P, PACK, T], F32, name="dy_raw%d" % g, align_bytes=64) for g in range(PASSES)]
+        dy_raw = [keep.tile([P, PACK, T], F32, name="dy_raw%d" % g, align_bytes=64) for g in range(PASSES - 1)]
+        dy_last = [keep.tile([P, PACK, N], F32, name="dy_last%d" % h, align_bytes=64) for h in range(HALVES)]
         res = [keep.tile([P, PACK, T], F32, name="res%d" % a, align_bytes=64) for a in range(BLOCKS)]
         dy_codes = {}
         dy_scales = {}
@@ -67,12 +68,11 @@ def tile_mix_dyq_fm_pl_res_kernel(
             for j in range(4):
                 nc.sync.dma_start(out=raw[j:P:32, :, :].bitcast(I32), in_=rows[j])
 
-        def load_dy(g):
-            rows = dy[g * K_PASS : (g + 1) * K_PASS, :]
-            nc.sync.dma_start(out=dy_raw[g][:], in_=rows.rearrange("(p j) t -> p j t", j=PACK))
-
         def rows_of(x, a):
             return x[a * K_PASS : (a + 1) * K_PASS, :].rearrange("(p j) t -> p j t", j=PACK)
+
+        def load_dy(g):
+            nc.sync.dma_start(out=dy_raw[g][:], in_=rows_of(dy, g))
 
         nc.vector.memset(s8_raw[:].bitcast(I32), 0)
         nc.vector.memset(s4_raw[:].bitcast(I32), 0)
@@ -82,8 +82,10 @@ def tile_mix_dyq_fm_pl_res_kernel(
         load_dy(0)
         nc.sync.dma_start(out=w4_raw[:].bitcast(I32), in_=w4_words.rearrange("a p n -> p a n").bitcast(I32))
         load_scales(s4_raw, w4_scales)
-        for g in range(1, PASSES):
+        for g in range(1, PASSES - 1):
             load_dy(g)
+        for h in range(HALVES):
+            nc.sync.dma_start(out=dy_last[h][:], in_=rows_of(dy, PASSES - 1)[:, :, h * N : (h + 1) * N])
         for a in range(BLOCKS):
             for j in (0, 2):
                 nc.sync.dma_start(out=res[a][:, j : j + 2, :], in_=rows_of(r, a)[:, j : j + 2, :])
@@ -106,22 +108,20 @@ def tile_mix_dyq_fm_pl_res_kernel(
                 in_=raw[:].rearrange("p a (b m j) -> p (a b) j m", j=PACK, m=P),
             )
 
-        def round_half(rows, h, vector_cols, run):
+        def round_half(rows, c0, vector_cols, run):
             grouped = stage.tile([P, N, PACK], BF16, name="grouped", align_bytes=64)
-            c0 = h * N
             if vector_cols > 0:
                 interleave(nc.vector.tensor_copy, grouped, rows, c0, c0 + vector_cols, c0, run)
-            interleave(nc.scalar.copy, grouped, rows, c0 + vector_cols, c0 + N, c0, run)
+            if vector_cols < N:
+                interleave(nc.scalar.copy, grouped, rows, c0 + vector_cols, c0 + N, c0, run)
             return grouped
 
-        def quantize_dy(g):
-            grouped = [round_half(dy_raw[g], h, VECTOR_COLS, RUN) for h in range(HALVES)]
-            for h in range(HALVES):
-                nc.vector.quantize_mx(
-                    out=dy_codes[g, h][:].bitcast(E5M2),
-                    scales=dy_scales[g, h][:],
-                    in_=grouped[h][:].rearrange("p c j -> p (c j)"),
-                )
+        def quantize_dy(grouped, g, h):
+            nc.vector.quantize_mx(
+                out=dy_codes[g, h][:].bitcast(E5M2),
+                scales=dy_scales[g, h][:],
+                in_=grouped[:].rearrange("p c j -> p (c j)"),
+            )
 
         def multiply(bank, a, j, h, g):
             col = (g % W_PASSES) * M + a * K_PASS + j * P
@@ -160,43 +160,51 @@ def tile_mix_dyq_fm_pl_res_kernel(
                 out=out_1[a].rearrange("p n i -> p (n i)").bitcast(I32), in_=out_codes[a][:].bitcast(I32)
             )
 
-        groups = [(j, h) for h in range(HALVES) for j in range(PACK)]
+        def new_bank(j, h):
+            return psum.tile([P, N], F32, name="bank%d%d" % (j, h))
 
         deal_w8()
         deal_scales(s8, s8_raw)
-        banks = [psum.tile([P, N], F32, name="bank%d" % n) for n in range(len(groups))]
-        for g in range(PASSES):
-            quantize_dy(g)
+        banks = {(j, h): new_bank(j, h) for h in range(HALVES) for j in range(PACK)}
+        for g in range(PASSES - 1):
+            grouped = [round_half(dy_raw[g], h * N, VECTOR_COLS, RUN) for h in range(HALVES)]
+            for h in range(HALVES):
+                quantize_dy(grouped[h], g, h)
+                for j in range(PACK):
+                    multiply(banks[j, h], 0, j, h, g)
             if g == 0:
                 deal_w4()
                 deal_scales(s4, s4_raw)
-            for n, (j, h) in enumerate(groups):
-                multiply(banks[n], 0, j, h, g)
+        for h in range(HALVES):
+            quantize_dy(round_half(dy_last[h], 0, VECTOR_COLS, RUN), PASSES - 1, h)
+            for j in range(PACK):
+                multiply(banks[j, h], 0, j, h, PASSES - 1)
 
+        order = [(j0 + j, h) for j0 in (0, 2) for h in range(HALVES) for j in range(2)]
         grouped = {}
-        later = []
-        for n, (j, h) in enumerate(groups):
-            add_residual(banks[n], 0, j, h)
+        later = {}
+        for j, h in order:
+            add_residual(banks[j, h], 0, j, h)
             if j == PACK - 1:
-                grouped[0, h] = round_half(res[0], h, 0, 1)
+                grouped[0, h] = round_half(res[0], h * N, 0, RUN if h == HALVES - 1 else 1)
             if h == HALVES - 1 and j % 2 == 1:
                 store_rows(0, j - 1)
-            bank = psum.tile([P, N], F32, name="bank%d" % n)
-            later.append(bank)
+            later[j, h] = new_bank(j, h)
             for g in range(PASSES):
-                multiply(bank, 1, j, h, g)
+                multiply(later[j, h], 1, j, h, g)
 
-        for n, (j, h) in enumerate(groups):
-            add_residual(later[n], 1, j, h)
-            if n == 3:
-                grouped[1, 0] = round_half(res[1], 0, 0, 1)
+        for j, h in order:
+            add_residual(later[j, h], 1, j, h)
+            if (j, h) == (1, 1):
+                store_rows(1, 0)
                 quantize_out(grouped[0, 0], 0, 0)
-            if n == 4:
+            if (j, h) == (3, 0):
+                grouped[1, 0] = round_half(res[1], 0, 0, 1)
+            if (j, h) == (2, 1):
                 quantize_out(grouped[0, 1], 0, 1)
                 store_codes(0)
-            if h == HALVES - 1 and j % 2 == 1:
-                store_rows(1, j - 1)
-        grouped[1, 1] = round_half(res[1], 1, 352, 1)
+        store_rows(1, 2)
+        grouped[1, 1] = round_half(res[1], N, N, RUN)
         quantize_out(grouped[1, 0], 1, 0)
         quantize_out(grouped[1, 1], 1, 1)
         for q in (0, 2, 1, 3):

@@ -148,16 +148,17 @@ def tile_mix_dyq_fm_pl_res_kernel(
         def quantize_out(grouped, a, h):
             nc.vector.quantize_mx(
                 out=out_codes[a][:, h * N : (h + 1) * N].bitcast(E4M3),
-                scales=out_scales[4 * a : P, h * N : (h + 1) * N],
+                scales=out_scales[4 + 4 * a : P, h * N : (h + 1) * N],
                 in_=grouped[:].rearrange("p c j -> p (c j)"),
             )
 
         def store_rows(a, j):
             nc.sync.dma_start(out=rows_of(out_0, a)[:, j : j + 2, :], in_=res[a][:, j : j + 2, :])
 
-        def store_codes(a):
+        def store_codes(a, c0, c1):
             nc.sync.dma_start(
-                out=out_1[a].rearrange("p n i -> p (n i)").bitcast(I32), in_=out_codes[a][:].bitcast(I32)
+                out=out_1[a, :, c0:c1, :].rearrange("p n i -> p (n i)").bitcast(I32),
+                in_=out_codes[a][:, c0:c1].bitcast(I32),
             )
 
         def new_bank(j, h):
@@ -202,14 +203,14 @@ def tile_mix_dyq_fm_pl_res_kernel(
                 grouped[1, 0] = round_half(res[1], 0, 0, 1)
             if (j, h) == (2, 1):
                 quantize_out(grouped[0, 1], 0, 1)
-                store_codes(0)
+                store_codes(0, 0, T)
         store_rows(1, 2)
         grouped[1, 1] = round_half(res[1], N, N, RUN)
-        quantize_out(grouped[1, 0], 1, 0)
-        quantize_out(grouped[1, 1], 1, 1)
+        for h in range(HALVES):
+            quantize_out(grouped[1, h], 1, h)
+            store_codes(1, h * N, (h + 1) * N)
         for q in (0, 2, 1, 3):
-            nc.sync.dma_start(
+            nc.scalar.dma_start(
                 out=out_2[:, 4 * q : 4 * q + 4, :].bitcast(I32),
-                in_=out_scales[32 * q : 32 * q + 8, :].bitcast(I32),
+                in_=out_scales[32 * q + 4 : 32 * q + 12, :].bitcast(I32),
             )
-        store_codes(1)

from contextlib import ExitStack

import concourse.mybir as mybir

O, K, M, T = 1024, 2048, 1024, 1024
FLOPS = 2 * K * M * T

F32 = mybir.dt.float32
BF16 = mybir.dt.bfloat16
I32 = mybir.dt.int32
U32 = mybir.dt.uint32
U8 = mybir.dt.uint8
E4M3 = mybir.dt.float8_e4m3fn_x4
E5M2 = mybir.dt.float8_e5m2_x4
E2M1 = mybir.dt.float4_e2m1fn_x4

P = 128
PACK = 4
K_PASS = P * PACK
N = 512
PASSES = K // K_PASS
W_PASSES = O // K_PASS
BLOCKS = M // K_PASS
HALVES = T // N
RUN = 4
VECTOR_COLS = 288


def interleave(copy, grouped, rows, c0, c1, g0, run):
    copy(
        out=grouped[:, c0 - g0 : c1 - g0, :].rearrange("p (c i) j -> p c j i", i=run),
        in_=rows[:, :, c0:c1].rearrange("p j (c i) -> p c j i", i=run),
    )


def tile_mix_dyq_fm_pl_res_kernel(
    tc, dy, w8_words, w8_scales, w4_words, w4_scales, r, out_0, out_1, out_2
):
    nc = tc.nc
    with ExitStack() as ctx:
        keep = ctx.enter_context(tc.tile_pool(name="keep", bufs=1))
        stage = ctx.enter_context(tc.tile_pool(name="stage", bufs=4))
        psum = ctx.enter_context(tc.psum_pool(name="psum", bufs=1))
        ctx.enter_context(tc.manual_schedule())

        w8_raw = keep.tile([P, W_PASSES, M], I32, align_bytes=64)
        w4_raw = keep.tile([P, W_PASSES, 2 * M], U8, align_bytes=64)
        s8_raw = keep.tile([P, W_PASSES, M], U8, align_bytes=64)
        s4_raw = keep.tile([P, W_PASSES, M], U8, align_bytes=64)
        w8 = keep.tile([P, W_PASSES * M], U32, align_bytes=64)
        w4 = keep.tile([P, W_PASSES * 2 * M], U8, align_bytes=64)
        s8 = keep.tile([P, W_PASSES * M], U8, align_bytes=64)
        s4 = keep.tile([P, W_PASSES * M], U8, align_bytes=64)
        dy_raw = [keep.tile([P, PACK, T], F32, name="dy_raw%d" % g, align_bytes=64) for g in range(PASSES - 1)]
        dy_last = [keep.tile([P, PACK, N], F32, name="dy_last%d" % h, align_bytes=64) for h in range(HALVES)]
        res = [keep.tile([P, PACK, T], F32, name="res%d" % a, align_bytes=64) for a in range(BLOCKS)]
        dy_codes = {}
        dy_scales = {}
        for g in range(PASSES):
            for h in range(HALVES):
                dy_codes[g, h] = keep.tile([P, N], U32, name="dy_codes%d%d" % (g, h), align_bytes=64)
                dy_scales[g, h] = keep.tile([P, N], U8, name="dy_scales%d%d" % (g, h), align_bytes=64)
        out_codes = [keep.tile([P, T], U32, name="out_codes%d" % a, align_bytes=64) for a in range(BLOCKS)]
        out_scales = keep.tile([P, T], U8, align_bytes=64)

        def load_scales(raw, scales):
            rows = scales.bitcast(I32).rearrange("a (q j) n -> j q a n", j=4)
            for j in range(4):
                nc.sync.dma_start(out=raw[j:P:32, :, :].bitcast(I32), in_=rows[j])

        def rows_of(x, a):
            return x[a * K_PASS : (a + 1) * K_PASS, :].rearrange("(p j) t -> p j t", j=PACK)

        def load_dy(g):
            nc.sync.dma_start(out=dy_raw[g][:], in_=rows_of(dy, g))

        nc.vector.memset(s8_raw[:].bitcast(I32), 0)
        nc.vector.memset(s4_raw[:].bitcast(I32), 0)

        nc.sync.dma_start(out=w8_raw[:], in_=w8_words.rearrange("a p n i -> p a (n i)").bitcast(I32))
        load_scales(s8_raw, w8_scales)
        load_dy(0)
        nc.sync.dma_start(out=w4_raw[:].bitcast(I32), in_=w4_words.rearrange("a p n -> p a n").bitcast(I32))
        load_scales(s4_raw, w4_scales)
        for g in range(1, PASSES - 1):
            load_dy(g)
        for h in range(HALVES):
            nc.sync.dma_start(out=dy_last[h][:], in_=rows_of(dy, PASSES - 1)[:, :, h * N : (h + 1) * N])
        for a in range(BLOCKS):
            for j in (0, 2):
                nc.sync.dma_start(out=res[a][:, j : j + 2, :], in_=rows_of(r, a)[:, j : j + 2, :])

        def deal_w8():
            nc.vector.tensor_copy(
                out=w8[:].bitcast(I32).rearrange("p (b j c i) -> p b c j i", j=PACK, i=RUN, c=P // RUN),
                in_=w8_raw[:].rearrange("p a (b c i j) -> p (a b) c j i", j=PACK, i=RUN, c=P // RUN),
            )

        def deal_w4():
            nc.vector.tensor_copy(
                out=w4[:].rearrange("p (b j m e) -> p b j m e", j=PACK, m=P, e=2),
                in_=w4_raw[:].rearrange("p a (b m j e) -> p (a b) j m e", j=PACK, m=P, e=2),
            )

        def deal_scales(dealt, raw):
            nc.vector.tensor_copy(
                out=dealt[:].rearrange("p (b j m) -> p b j m", j=PACK, m=P),
                in_=raw[:].rearrange("p a (b m j) -> p (a b) j m", j=PACK, m=P),
            )

        def round_half(rows, c0, vector_cols, run):
            grouped = stage.tile([P, N, PACK], BF16, name="grouped", align_bytes=64)
            if vector_cols > 0:
                interleave(nc.vector.tensor_copy, grouped, rows, c0, c0 + vector_cols, c0, run)
            if vector_cols < N:
                interleave(nc.scalar.copy, grouped, rows, c0 + vector_cols, c0 + N, c0, run)
            return grouped

        def quantize_dy(grouped, g, h):
            nc.vector.quantize_mx(
                out=dy_codes[g, h][:].bitcast(E5M2),
                scales=dy_scales[g, h][:],
                in_=grouped[:].rearrange("p c j -> p (c j)"),
            )

        def multiply(bank, a, j, h, g):
            col = (g % W_PASSES) * M + a * K_PASS + j * P
            if g < W_PASSES:
                lhsT = w8[:, col : col + P].bitcast(E4M3)
                lhsT_scale = s8[:, col : col + P]
            else:
                lhsT = w4[:, 2 * col : 2 * (col + P)].bitcast(E2M1)
                lhsT_scale = s4[:, col : col + P]
            nc.tensor.matmul_mx(
                out=bank[:],
                lhsT=lhsT,
                lhsT_scale=lhsT_scale,
                rhs=dy_codes[g, h][:].bitcast(E5M2),
                rhs_scale=dy_scales[g, h][:],
                start=(g == 0),
                stop=(g == PASSES - 1),
            )

        def add_residual(bank, a, j, h):
            part = res[a][:, j, h * N : (h + 1) * N]
            nc.vector.tensor_tensor(out=part, in0=bank[:], in1=part, op=mybir.AluOpType.add)

        def quantize_out(grouped, a, h):
            nc.vector.quantize_mx(
                out=out_codes[a][:, h * N : (h + 1) * N].bitcast(E4M3),
                scales=out_scales[4 + 4 * a : P, h * N : (h + 1) * N],
                in_=grouped[:].rearrange("p c j -> p (c j)"),
            )

        def store_rows(a, j):
            nc.sync.dma_start(out=rows_of(out_0, a)[:, j : j + 2, :], in_=res[a][:, j : j + 2, :])

        def store_codes(a, c0, c1):
            nc.sync.dma_start(
                out=out_1[a, :, c0:c1, :].rearrange("p n i -> p (n i)").bitcast(I32),
                in_=out_codes[a][:, c0:c1].bitcast(I32),
            )

        def new_bank(j, h):
            return psum.tile([P, N], F32, name="bank%d%d" % (j, h))

        deal_w8()
        deal_scales(s8, s8_raw)
        banks = {(j, h): new_bank(j, h) for h in range(HALVES) for j in range(PACK)}
        for g in range(PASSES - 1):
            grouped = [round_half(dy_raw[g], h * N, VECTOR_COLS, RUN) for h in range(HALVES)]
            for h in range(HALVES):
                quantize_dy(grouped[h], g, h)
                for j in range(PACK):
                    multiply(banks[j, h], 0, j, h, g)
            if g == 0:
                deal_w4()
                deal_scales(s4, s4_raw)
        for h in range(HALVES):
            quantize_dy(round_half(dy_last[h], 0, VECTOR_COLS, RUN), PASSES - 1, h)
            for j in range(PACK):
                multiply(banks[j, h], 0, j, h, PASSES - 1)

        order = [(j0 + j, h) for j0 in (0, 2) for h in range(HALVES) for j in range(2)]
        grouped = {}
        later = {}
        for j, h in order:
            add_residual(banks[j, h], 0, j, h)
            if j == PACK - 1:
                grouped[0, h] = round_half(res[0], h * N, 0, RUN if h == HALVES - 1 else 1)
            if h == HALVES - 1 and j % 2 == 1:
                store_rows(0, j - 1)
            later[j, h] = new_bank(j, h)
            for g in range(PASSES):
                multiply(later[j, h], 1, j, h, g)

        for j, h in order:
            add_residual(later[j, h], 1, j, h)
            if (j, h) == (1, 1):
                store_rows(1, 0)
                quantize_out(grouped[0, 0], 0, 0)
            if (j, h) == (3, 0):
                grouped[1, 0] = round_half(res[1], 0, 0, 1)
            if (j, h) == (2, 1):
                quantize_out(grouped[0, 1], 0, 1)
                store_codes(0, 0, T)
        store_rows(1, 2)
        grouped[1, 1] = round_half(res[1], N, N, RUN)
        for h in range(HALVES):
            quantize_out(grouped[1, h], 1, h)
            store_codes(1, h * N, (h + 1) * N)
        for q in (0, 2, 1, 3):
            nc.scalar.dma_start(
                out=out_2[:, 4 * q : 4 * q + 4, :].bitcast(I32),
                in_=out_scales[32 * q + 4 : 32 * q + 12, :].bitcast(I32),
            )
